import numpy as np
import ml_dtypes


def mxq(x, axis, fmt="e4m3"):
    dtype, down = {"e4m3": (ml_dtypes.float8_e4m3fn, 7), "e5m2": (ml_dtypes.float8_e5m2, 14)}[fmt]
    v = np.moveaxis(np.asarray(x, np.float32).astype(ml_dtypes.bfloat16).astype(np.float64), axis, -1)
    blocks = v.reshape(v.shape[:-1] + (-1, 32))
    amax = np.abs(blocks).max(-1, keepdims=True)
    byte = np.maximum(np.where(amax > 0, np.frexp(amax)[1] - 1 + 127, 0) - down, 1)
    scale = np.exp2(byte - 127.0)
    codes = (blocks / scale).astype(np.float32).astype(dtype).astype(np.float64)
    return np.moveaxis((codes * scale).reshape(v.shape), -1, axis)


WIDE = False


def mx_kscale(k):
    if not WIDE:
        return np.ones(k)
    levels = np.array([10, -10, 5, -5, 0])
    if k % 512:
        return np.exp2(np.random.permutation(np.resize(levels, k // 32))).repeat(32)
    a = np.empty((k // 512, 16))
    for p in range(k // 512):
        a[p, :8] = np.random.permutation(np.resize(levels, 8))
        for g in range(8):
            far = levels[np.abs(levels - a[p, g]) >= 10]
            a[p, g + 8] = far[np.random.randint(len(far))]
    return np.exp2(a.ravel()).repeat(32)


def f64(x):
    return np.asarray(x).astype(np.float64)


def striped(idx):
    return np.tile(idx.reshape(-1, 16).T, (8, 1)).astype(np.uint16)


def unstriped(offs):
    return offs[:16].T.reshape(-1).astype(np.int64)


def striped8(idx):
    return np.concatenate([x.reshape(-1, 16).T for x in idx]).astype(np.uint16)


def runs(offs, k):
    lists = np.stack([offs[16 * r : 16 * r + 16].T.reshape(-1) for r in range(8)]).astype(np.int64)
    return lists[np.arange(k) % 512 // 64]


def pack_weight(w):
    k, n = w.shape
    w = f64(np.asarray(w, np.float32).astype(ml_dtypes.bfloat16)).reshape(k // 32, 32, n)
    amax = np.abs(w).max(1)
    byte = np.clip(np.where(amax > 0, np.frexp(amax)[1] - 1 + 127 - 7, 1), 1, 254)
    scaled = (w * np.exp2(127.0 - byte)[:, None, :]).reshape(k, n).astype(np.float32)
    words = np.ascontiguousarray(scaled.reshape(k // 512, 128, 4, n).transpose(0, 1, 3, 2)).astype(ml_dtypes.float8_e4m3fn).view(np.uint8)
    return words, np.ascontiguousarray(byte.astype(np.uint8).reshape(k // 512, 16, n))


def unpack_weight(words, scales):
    g, p, n, _ = words.shape
    vals = np.ascontiguousarray(words).view(ml_dtypes.float8_e4m3fn).astype(np.float64) * np.repeat(np.exp2(scales.astype(np.float64) - 127.0), 8, axis=1)[..., None]
    return vals.transpose(0, 1, 3, 2).reshape(g * 512, n)


def sigmoid(v):
    return 1.0 / (1.0 + np.exp(-np.maximum(v, -700.0)))


K, T, S, N, G, H = 512, 1024, 512, 512, 2048, 512


def setup_inputs():
    n = np.random.standard_normal
    s = mx_kscale(K)[:, None]
    u = mx_kscale(S)
    packed_xT = pack_weight(n((K, T)) * s)
    packed_dT = pack_weight(n((K, G)) / s)
    return {
        "x_words": packed_xT[0],
        "x_scales": packed_xT[1],
        "d_words": packed_dT[0],
        "d_scales": packed_dT[1],
        "sl": np.random.uniform(1.0, 2.0, (H, 1)).astype(np.float32),
        "th": (0.5 * n((H, 1))).astype(np.float32),
        "sl2": np.random.uniform(1.0, 2.0, (H, 1)).astype(np.float32),
        "th2": (0.5 * n((H, 1))).astype(np.float32),
        "gn": (np.random.uniform(0.5, 1.5, (H, 1)) * u[:, None]).astype(np.float32),
        "w1": (n((H, N)) / np.sqrt(H) / u[:, None]).astype(np.float32),
        "tau": np.random.uniform(0.3, 0.9, (N, 1)).astype(np.float32),
        "offs": striped(np.random.permutation(T)[:S]),
        "k1": striped8(np.random.randint(0, G, (8, H))),
        "two": striped(np.random.permutation(T)[:S]),
        "k2": striped8(np.random.randint(0, G, (8, H))),
        "n1": striped(np.random.permutation(S)),
        "n2": striped(np.random.permutation(S)),
        "n3": striped8(np.stack([np.random.permutation(S) for _ in range(8)])),
        "n4": striped8(np.stack([np.random.permutation(S) for _ in range(8)])),
    }


def reference(x_words, x_scales, d_words, d_scales, sl, th, sl2, th2, gn, w1, tau, offs, k1, two, k2, n1, n2, n3, n4):
    d_k1 = unpack_weight(d_words, d_scales)[np.arange(K)[:, None], runs(k1, K)]
    xq = unpack_weight(x_words, x_scales)[:, unstriped(offs)]
    a = 0.0625 * (d_k1.T @ xq)
    sg = sigmoid(f64(sl) * (a[:, unstriped(n1)] - f64(th)))
    d_k2 = unpack_weight(d_words, d_scales)[np.arange(K)[:, None], runs(k2, K)]
    x_two = unpack_weight(x_words, x_scales)[:, unstriped(two)]
    b = 0.0625 * (d_k2.T @ x_two)
    sg2 = sigmoid(f64(sl2) * (b[:, unstriped(n2)] - f64(th2)))
    z = f64(gn) * (sg * b + sg2 * a)
    h = mxq(f64(w1), 0, "e4m3").T @ mxq(z, 0, "e4m3")
    top = h.max(axis=1, keepdims=True)
    ea = np.exp(f64(tau) * (h[np.arange(N)[:, None], runs(n3, N)] - top))
    ea2 = np.exp(f64(tau) * (h[np.arange(N)[:, None], runs(n4, N)] - top))
    return h + np.log(ea + ea2 + 0.25)

@@ -1,0 +1,238 @@
+from contextlib import ExitStack
+
+import concourse.mybir as mybir
+
+K, T, S, N, G, H = 512, 1024, 512, 512, 2048, 512
+FLOPS = 2 * K * H * S * 2 + 2 * H * N * S
+
+F32 = mybir.dt.float32
+BF16 = mybir.dt.bfloat16
+I32 = mybir.dt.int32
+U32 = mybir.dt.uint32
+U16 = mybir.dt.uint16
+U8 = mybir.dt.uint8
+FP8X4 = mybir.dt.float8_e4m3fn_x4
+ALU = mybir.AluOpType
+ACT = mybir.ActivationFunctionType
+
+P = 128
+PACK = 4
+HALF = S // 2
+LIST_COLS = S // 16
+HALVES = (0, 1)
+
+
+def tile_picked_twpqcxbelg_none_p_kernel(
+    tc, x_words, x_scales, d_words, d_scales, sl, th, sl2, th2, gn, w1, tau,
+    offs, k1, two, k2, n1, n2, n3, n4, out,
+):
+    nc = tc.nc
+    with ExitStack() as ctx:
+        lists = ctx.enter_context(tc.tile_pool(name="lists", bufs=1))
+        keep = ctx.enter_context(tc.tile_pool(name="keep", bufs=1))
+        reuse = ctx.enter_context(tc.tile_pool(name="reuse", bufs=1))
+        psum = ctx.enter_context(tc.psum_pool(name="psum", bufs=1))
+
+        def load_list(name, source):
+            tile = lists.tile([P, LIST_COLS], U16, name=name)
+            nc.sync.dma_start(tile[:], source)
+            return tile
+
+        def half_cols(half):
+            return slice(half * HALF, (half + 1) * HALF)
+
+        def half_list(tile, half):
+            return tile[:, half * LIST_COLS // 2 : (half + 1) * LIST_COLS // 2]
+
+        d_byte_table = keep.tile([P, G], U8, name="d_byte_table", align_bytes=64)
+        x_byte_table = keep.tile([P, T], U8, name="x_byte_table", align_bytes=64)
+        d_word_table = keep.tile([P, G], U32, name="d_word_table", align_bytes=64)
+        x_word_table = keep.tile([P, T], U32, name="x_word_table", align_bytes=64)
+        k1_list = load_list("k1_list", k1)
+        nc.sync.dma_start(
+            d_byte_table[:].bitcast(I32), d_scales[0].bitcast(I32).unsqueeze(1).to_broadcast([16, 8, G // 4])
+        )
+        offs_list = load_list("offs_list", offs)
+        nc.sync.dma_start(
+            x_byte_table[:].bitcast(I32), x_scales[0].bitcast(I32).unsqueeze(1).to_broadcast([16, 8, T // 4])
+        )
+        nc.sync.dma_start(x_word_table[:].bitcast(I32), x_words[0].rearrange("p n t -> p (n t)").bitcast(I32))
+        nc.sync.dma_start(d_word_table[:].bitcast(I32), d_words[0].rearrange("p n t -> p (n t)").bitcast(I32))
+        k2_list = load_list("k2_list", k2)
+        two_list = load_list("two_list", two)
+        n1_list = load_list("n1_list", n1)
+        n2_list = load_list("n2_list", n2)
+        n3_list = load_list("n3_list", n3)
+        n4_list = load_list("n4_list", n4)
+
+        def load_rows(name, source):
+            tile = keep.tile([P, PACK], F32, name=name)
+            nc.gpsimd.dma_start(tile[:], source.rearrange("(p t) o -> p (t o)", t=PACK))
+            return tile
+
+        def times(name, tile, factor):
+            result = keep.tile([P, PACK], F32, name=name)
+            nc.gpsimd.tensor_scalar(result[:], tile[:], factor, 0.0, ALU.mult, ALU.add)
+            return result
+
+        def sigmoid_bias(name, slope, threshold):
+            minus = times(name + "_minus", threshold, -1.0)
+            result = keep.tile([P, PACK], F32, name=name)
+            nc.gpsimd.tensor_tensor(result[:], slope[:], minus[:], ALU.mult)
+            return result
+
+        sl_rows = load_rows("sl_rows", sl)
+        th_rows = load_rows("th_rows", th)
+        bias_a = sigmoid_bias("bias_a", sl_rows, th_rows)
+        sl2_rows = load_rows("sl2_rows", sl2)
+        th2_rows = load_rows("th2_rows", th2)
+        bias_b = sigmoid_bias("bias_b", sl2_rows, th2_rows)
+        gn_rows = load_rows("gn_rows", gn)
+        gain = times("gain", gn_rows, 0.0625)
+        tau_rows = load_rows("tau_rows", tau)
+        minus_tau = times("minus_tau", tau_rows, -1.0)
+
+        def coded_product(name, d_list, x_list, picked, d_picked, x_picked, bank_tag):
+            placed = keep.tile([P, H + S], U8, name=name + "_placed", align_bytes=64)
+            nc.vector.memset(placed[:].bitcast(I32), 0)
+            dealt = keep.tile([P, H + S], U8, name=name + "_dealt", tag=name + "_dealt", align_bytes=64)
+            d_dealt = keep.tile([P, H], U32, name=name + "_d_dealt", align_bytes=64)
+            nc.vector.tensor_copy(picked[:, 0:H], d_byte_table[:].indirect(d_list[:]))
+            nc.vector.tensor_copy(picked[:, H : H + S], x_byte_table[:].indirect(x_list[:]))
+            nc.vector.tensor_copy(
+                dealt[:, 0:H].rearrange("p (t c i) -> p c t i", t=PACK, i=16),
+                picked[:, 0:H].rearrange("p (c i t) -> p c t i", t=PACK, i=16),
+            )
+            nc.vector.tensor_copy(dealt[:, H : H + S].bitcast(I32), picked[:, H : H + S].bitcast(I32))
+            for r in range(4):
+                nc.sync.dma_start(placed[r:P:32, :].bitcast(I32), dealt[8 * r : P : 32, :].bitcast(I32))
+            nc.vector.tensor_copy(x_picked[:], x_word_table[:].indirect(x_list[:]))
+            nc.vector.tensor_copy(d_picked[:], d_word_table[:].indirect(d_list[:]))
+            nc.vector.tensor_copy(
+                d_dealt[:].bitcast(I32).rearrange("p (t c i) -> p c t i", t=PACK, i=4),
+                d_picked[:].bitcast(I32).rearrange("p (c i t) -> p c t i", t=PACK, i=4),
+            )
+            banks = []
+            for t in range(PACK):
+                bank = psum.tile([P, S], F32, name=name + "_sums%d" % t, tag=bank_tag + "%d" % t)
+                cols = slice(t * P, (t + 1) * P)
+                nc.tensor.matmul_mx(
+                    out=bank[:],
+                    lhsT=d_dealt[:, cols].bitcast(FP8X4), lhsT_scale=placed[:, cols],
+                    rhs=x_picked[:].bitcast(FP8X4), rhs_scale=placed[:, H : H + S],
+                    start=True, stop=True,
+                )
+                banks.append(bank)
+            return banks
+
+        a_picked = keep.tile([P, H + S], U8, name="a_picked", align_bytes=64)
+        a_x_picked = keep.tile([P, S], U32, name="a_x_picked", align_bytes=64)
+        a_d_picked = reuse.tile([P, H], U32, name="a_d_picked", align_bytes=64, offset=2048)
+        a_banks = coded_product("a", k1_list, offs_list, a_picked, a_d_picked, a_x_picked, "first")
+
+        sg = []
+        for t in range(PACK):
+            a_rows = keep.tile([P, S], F32, name="a_rows%d" % t)
+            nc.scalar.activation(a_rows[:], a_banks[t][:], ACT.Copy, scale=0.0625)
+            gate = keep.tile([P, S], F32, name="sg%d" % t)
+            for half in HALVES:
+                nc.scalar.activation(
+                    gate[:, half_cols(half)], a_rows[:].indirect(half_list(n1_list, half)), ACT.Sigmoid,
+                    bias=bias_a[:, t : t + 1], scale=sl_rows[:, t : t + 1],
+                )
+            sg.append(gate)
+
+        b_d_picked = reuse.tile([P, H], U32, name="b_d_picked", align_bytes=64, offset=256)
+        b_picked = reuse.tile([P, H + S], U8, name="b_picked", align_bytes=64, offset=2304)
+        b_x_picked = reuse.tile([P, S], U32, name="b_x_picked", align_bytes=64, offset=3328)
+        b_banks = coded_product("b", k2_list, two_list, b_picked, b_d_picked, b_x_picked, "second")
+
+        w_raw = keep.tile([P, PACK, N], F32, name="w_raw", tag="a_dealt", align_bytes=64)
+        nc.sync.dma_start(w_raw[:], w1.rearrange("(p j) m -> p j m", j=PACK))
+        w_grouped = keep.tile([P, N * PACK], BF16, name="w_grouped", align_bytes=64)
+        nc.vector.tensor_copy(
+            w_grouped[:].rearrange("p (t m j) -> p m j t", t=PACK, j=PACK),
+            w_raw[:].rearrange("p j (m t) -> p m j t", t=PACK),
+        )
+
+        b_rows = [keep.tile([P, S], F32, name="b_rows%d" % t) for t in range(PACK)]
+        for t in range(2):
+            nc.vector.tensor_scalar(b_rows[t][:], b_banks[t][:], 0.0625, None, ALU.mult)
+        w_codes = keep.tile([P, N], U32, name="w_codes", align_bytes=64)
+        w_bytes = keep.tile([P, N], U8, name="w_bytes", align_bytes=64)
+        nc.vector.quantize_mx(out=w_codes[:].bitcast(FP8X4), scales=w_bytes[:], in_=w_grouped[:])
+
+        first_term = keep.tile([P, PACK, S], F32, name="first_term")
+        for t in range(PACK):
+            nc.vector.scalar_tensor_tensor(
+                first_term[:, t, :], b_banks[t][:], gain[:, t : t + 1], sg[t][:], ALU.mult, ALU.mult
+            )
+
+        h_banks = [psum.tile([P, S], F32, name="h_sums%d" % t, tag="second%d" % t) for t in range(PACK)]
+        for half in HALVES:
+            cols = half_cols(half)
+            second_term = keep.tile([P, PACK, HALF], F32, name="second_term%d" % half)
+            for t in range(PACK):
+                if half == 0 and t >= 2:
+                    nc.scalar.activation(b_rows[t][:], b_banks[t][:], ACT.Copy, scale=0.0625)
+                gate = keep.tile([P, HALF], F32, name="sg2_%d_%d" % (half, t))
+                nc.scalar.activation(
+                    gate[:], b_rows[t][:].indirect(half_list(n2_list, half)), ACT.Sigmoid,
+                    bias=bias_b[:, t : t + 1], scale=sl2_rows[:, t : t + 1],
+                )
+                nc.vector.scalar_tensor_tensor(
+                    second_term[:, t, :], a_banks[t][:, cols], gain[:, t : t + 1], gate[:], ALU.mult, ALU.mult
+                )
+            z_grouped = keep.tile([P, HALF * PACK], BF16, name="z_grouped%d" % half, align_bytes=64)
+            nc.vector.tensor_tensor(
+                z_grouped[:].rearrange("p (c i t) -> p c t i", t=PACK, i=4),
+                first_term[:, :, cols].rearrange("p t (c i) -> p c t i", i=4),
+                second_term[:].rearrange("p t (c i) -> p c t i", i=4),
+                ALU.add,
+            )
+            z_codes = keep.tile([P, HALF], U32, name="z_codes%d" % half, align_bytes=64)
+            z_bytes = keep.tile([P, HALF], U8, name="z_bytes%d" % half, align_bytes=64)
+            nc.vector.quantize_mx(out=z_codes[:].bitcast(FP8X4), scales=z_bytes[:], in_=z_grouped[:])
+            for t in range(PACK):
+                rows = slice(t * P, (t + 1) * P)
+                nc.tensor.matmul_mx(
+                    out=h_banks[t][:, cols],
+                    lhsT=w_codes[:, rows].bitcast(FP8X4), lhsT_scale=w_bytes[:, rows],
+                    rhs=z_codes[:].bitcast(FP8X4), rhs_scale=z_bytes[:],
+                    start=True, stop=True,
+                )
+
+        h_rows, exp_bias = [], []
+        for t in range(PACK):
+            rows = keep.tile([P, S], F32, name="h_rows%d" % t)
+            top = keep.tile([P, 1], F32, name="top%d" % t)
+            nc.vector.tensor_scalar(rows[:], h_banks[t][:], 1.0, None, ALU.mult, ALU.max, accum_out=top[:])
+            bias = keep.tile([P, 1], F32, name="exp_bias%d" % t)
+            nc.vector.tensor_tensor(bias[:], top[:], minus_tau[:, t : t + 1], ALU.mult)
+            h_rows.append(rows)
+            exp_bias.append(bias)
+
+        sums = []
+        for t in range(PACK):
+            pair = []
+            for which, place_list in enumerate((n3_list, n4_list)):
+                fetched = keep.tile([P, S], F32, name="ea%d_%d" % (which, t))
+                for half in HALVES:
+                    nc.scalar.activation(
+                        fetched[:, half_cols(half)], h_rows[t][:].indirect(half_list(place_list, half)), ACT.Exp,
+                        bias=exp_bias[t][:], scale=tau_rows[:, t : t + 1],
+                    )
+                pair.append(fetched)
+            total = keep.tile([P, S], F32, name="total%d" % t)
+            nc.vector.tensor_tensor(total[:], pair[0][:], pair[1][:], ALU.add)
+            sums.append(total)
+
+        out_rows = out.rearrange("(p t) j -> p t j", t=PACK)
+        pieces = [(t, slice(0, S)) for t in range(PACK - 1)] + [(PACK - 1, half_cols(half)) for half in HALVES]
+        for number, (t, cols) in enumerate(pieces):
+            width = cols.stop - cols.start
+            logs = keep.tile([P, width], F32, name="logs%d" % number)
+            nc.scalar.activation(logs[:], sums[t][:, cols], ACT.Ln, bias=0.25)
+            result = keep.tile([P, width], F32, name="result%d" % number)
+            nc.vector.tensor_tensor(result[:], logs[:], h_rows[t][:, cols], ALU.add)
+            nc.sync.dma_start(out_rows[:, t, cols], result[:])

@@ -38,11 +38,25 @@ def tile_picked_twpqcxbelg_none_p_kernel(
             nc.sync.dma_start(tile[:], source)
             return tile
 
+        w_raw = [
+            reuse.tile([P, PACK, N // 2], F32, name="w_raw0", offset=12288),
+            keep.tile([P, PACK, N // 2], F32, name="w_raw1"),
+        ]
+
+        def load_w1(half):
+            columns = slice(half * N // 2, (half + 1) * N // 2)
+            nc.sync.dma_start(w_raw[half][:], w1.rearrange("(p j) m -> p j m", j=PACK)[:, :, columns])
+
         def half_cols(half):
             return slice(half * HALF, (half + 1) * HALF)
 
         def half_list(tile, half):
             return tile[:, half * LIST_COLS // 2 : (half + 1) * LIST_COLS // 2]
+
+        warm_in = keep.tile([P, 1], F32, name="warm_in")
+        warm_out = keep.tile([P, 1], F32, name="warm_out")
+        nc.vector.memset(warm_in[:], 0.0)
+        nc.scalar.activation(warm_out[:], warm_in[:], ACT.Sigmoid)
 
         d_byte_table = keep.tile([P, G], U8, name="d_byte_table", align_bytes=64)
         x_byte_table = keep.tile([P, T], U8, name="x_byte_table", align_bytes=64)
@@ -57,6 +71,7 @@ def tile_picked_twpqcxbelg_none_p_kernel(
             x_byte_table[:].bitcast(I32), x_scales[0].bitcast(I32).unsqueeze(1).to_broadcast([16, 8, T // 4])
         )
         nc.sync.dma_start(x_word_table[:].bitcast(I32), x_words[0].rearrange("p n t -> p (n t)").bitcast(I32))
+        load_w1(0)
         nc.sync.dma_start(d_word_table[:].bitcast(I32), d_words[0].rearrange("p n t -> p (n t)").bitcast(I32))
         k2_list = load_list("k2_list", k2)
         two_list = load_list("two_list", two)
@@ -64,6 +79,16 @@ def tile_picked_twpqcxbelg_none_p_kernel(
         n2_list = load_list("n2_list", n2)
         n3_list = load_list("n3_list", n3)
         n4_list = load_list("n4_list", n4)
+        load_w1(1)
+        w_grouped = keep.tile([P, N * PACK], BF16, name="w_grouped", align_bytes=64)
+
+        def group_w1(copy, half):
+            copy(
+                w_grouped[:].rearrange("p (t h m j) -> p h m j t", t=PACK, h=2, j=PACK)[:, half],
+                w_raw[half][:].rearrange("p j (m t) -> p m j t", t=PACK),
+            )
+
+        group_w1(nc.scalar.copy, 0)
 
         def load_rows(name, source):
             tile = keep.tile([P, PACK], F32, name=name)
@@ -92,10 +117,10 @@ def tile_picked_twpqcxbelg_none_p_kernel(
         tau_rows = load_rows("tau_rows", tau)
         minus_tau = times("minus_tau", tau_rows, -1.0)
 
-        def coded_product(name, d_list, x_list, picked, d_picked, x_picked, bank_tag):
+        def coded_product(name, d_list, x_list, picked, d_picked, x_picked, bank_tag, queue):
             placed = keep.tile([P, H + S], U8, name=name + "_placed", align_bytes=64)
             nc.vector.memset(placed[:].bitcast(I32), 0)
-            dealt = keep.tile([P, H + S], U8, name=name + "_dealt", tag=name + "_dealt", align_bytes=64)
+            dealt = keep.tile([P, H + S], U8, name=name + "_dealt", align_bytes=64)
             d_dealt = keep.tile([P, H], U32, name=name + "_d_dealt", align_bytes=64)
             nc.vector.tensor_copy(picked[:, 0:H], d_byte_table[:].indirect(d_list[:]))
             nc.vector.tensor_copy(picked[:, H : H + S], x_byte_table[:].indirect(x_list[:]))
@@ -105,7 +130,7 @@ def tile_picked_twpqcxbelg_none_p_kernel(
             )
             nc.vector.tensor_copy(dealt[:, H : H + S].bitcast(I32), picked[:, H : H + S].bitcast(I32))
             for r in range(4):
-                nc.sync.dma_start(placed[r:P:32, :].bitcast(I32), dealt[8 * r : P : 32, :].bitcast(I32))
+                queue.dma_start(placed[r:P:32, :].bitcast(I32), dealt[8 * r : P : 32, :].bitcast(I32))
             nc.vector.tensor_copy(x_picked[:], x_word_table[:].indirect(x_list[:]))
             nc.vector.tensor_copy(d_picked[:], d_word_table[:].indirect(d_list[:]))
             nc.vector.tensor_copy(
@@ -128,13 +153,13 @@ def tile_picked_twpqcxbelg_none_p_kernel(
         a_picked = keep.tile([P, H + S], U8, name="a_picked", align_bytes=64)
         a_x_picked = keep.tile([P, S], U32, name="a_x_picked", align_bytes=64)
         a_d_picked = reuse.tile([P, H], U32, name="a_d_picked", align_bytes=64, offset=2048)
-        a_banks = coded_product("a", k1_list, offs_list, a_picked, a_d_picked, a_x_picked, "first")
+        a_banks = coded_product("a", k1_list, offs_list, a_picked, a_d_picked, a_x_picked, "first", nc.scalar)
 
         sg = []
         for t in range(PACK):
-            a_rows = keep.tile([P, S], F32, name="a_rows%d" % t)
+            a_rows = reuse.tile([P, S], F32, name="a_rows%d" % t, offset=12288 + 4 * S * t)
             nc.scalar.activation(a_rows[:], a_banks[t][:], ACT.Copy, scale=0.0625)
-            gate = keep.tile([P, S], F32, name="sg%d" % t)
+            gate = keep.tile([P, S], F32, name="sg%d" % t, tag="sg%d" % t)
             for half in HALVES:
                 nc.scalar.activation(
                     gate[:, half_cols(half)], a_rows[:].indirect(half_list(n1_list, half)), ACT.Sigmoid,
@@ -145,24 +170,18 @@ def tile_picked_twpqcxbelg_none_p_kernel(
         b_d_picked = reuse.tile([P, H], U32, name="b_d_picked", align_bytes=64, offset=256)
         b_picked = reuse.tile([P, H + S], U8, name="b_picked", align_bytes=64, offset=2304)
         b_x_picked = reuse.tile([P, S], U32, name="b_x_picked", align_bytes=64, offset=3328)
-        b_banks = coded_product("b", k2_list, two_list, b_picked, b_d_picked, b_x_picked, "second")
-
-        w_raw = keep.tile([P, PACK, N], F32, name="w_raw", tag="a_dealt", align_bytes=64)
-        nc.sync.dma_start(w_raw[:], w1.rearrange("(p j) m -> p j m", j=PACK))
-        w_grouped = keep.tile([P, N * PACK], BF16, name="w_grouped", align_bytes=64)
-        nc.vector.tensor_copy(
-            w_grouped[:].rearrange("p (t m j) -> p m j t", t=PACK, j=PACK),
-            w_raw[:].rearrange("p j (m t) -> p m j t", t=PACK),
-        )
+        b_banks = coded_product("b", k2_list, two_list, b_picked, b_d_picked, b_x_picked, "second", nc.sync)
 
         b_rows = [keep.tile([P, S], F32, name="b_rows%d" % t) for t in range(PACK)]
-        for t in range(2):
-            nc.vector.tensor_scalar(b_rows[t][:], b_banks[t][:], 0.0625, None, ALU.mult)
+        group_w1(nc.vector.tensor_copy, 1)
         w_codes = keep.tile([P, N], U32, name="w_codes", align_bytes=64)
         w_bytes = keep.tile([P, N], U8, name="w_bytes", align_bytes=64)
         nc.vector.quantize_mx(out=w_codes[:].bitcast(FP8X4), scales=w_bytes[:], in_=w_grouped[:])
+        for t in range(PACK - 1):
+            nc.vector.tensor_scalar(b_rows[t][:], b_banks[t][:], 0.0625, None, ALU.mult)
+        nc.scalar.activation(b_rows[PACK - 1][:], b_banks[PACK - 1][:], ACT.Copy, scale=0.0625)
 
-        first_term = keep.tile([P, PACK, S], F32, name="first_term")
+        first_term = reuse.tile([P, PACK, S], F32, name="first_term", offset=3328)
         for t in range(PACK):
             nc.vector.scalar_tensor_tensor(
                 first_term[:, t, :], b_banks[t][:], gain[:, t : t + 1], sg[t][:], ALU.mult, ALU.mult
@@ -171,11 +190,11 @@ def tile_picked_twpqcxbelg_none_p_kernel(
         h_banks = [psum.tile([P, S], F32, name="h_sums%d" % t, tag="second%d" % t) for t in range(PACK)]
         for half in HALVES:
             cols = half_cols(half)
-            second_term = keep.tile([P, PACK, HALF], F32, name="second_term%d" % half)
+            second_term = keep.tile(
+                [P, PACK, HALF], F32, name="second_term%d" % half, tag="stage%d" % half, align_bytes=64
+            )
             for t in range(PACK):
-                if half == 0 and t >= 2:
-                    nc.scalar.activation(b_rows[t][:], b_banks[t][:], ACT.Copy, scale=0.0625)
-                gate = keep.tile([P, HALF], F32, name="sg2_%d_%d" % (half, t))
+                gate = keep.tile([P, HALF], F32, name="sg2_%d_%d" % (half, t), tag=("sg2_%d", "sg%d")[half] % t)
                 nc.scalar.activation(
                     gate[:], b_rows[t][:].indirect(half_list(n2_list, half)), ACT.Sigmoid,
                     bias=bias_b[:, t : t + 1], scale=sl2_rows[:, t : t + 1],
@@ -183,7 +202,7 @@ def tile_picked_twpqcxbelg_none_p_kernel(
                 nc.vector.scalar_tensor_tensor(
                     second_term[:, t, :], a_banks[t][:, cols], gain[:, t : t + 1], gate[:], ALU.mult, ALU.mult
                 )
-            z_grouped = keep.tile([P, HALF * PACK], BF16, name="z_grouped%d" % half, align_bytes=64)
+            z_grouped = keep.tile([P, HALF * PACK], BF16, name="z_grouped%d" % half, tag="stage%d" % (half + 1), align_bytes=64)
             nc.vector.tensor_tensor(
                 z_grouped[:].rearrange("p (c i t) -> p c t i", t=PACK, i=4),
                 first_term[:, :, cols].rearrange("p t (c i) -> p c t i", i=4),

@@ -62,13 +62,13 @@ def tile_picked_twpqcxbelg_none_p_kernel(
         x_byte_table = keep.tile([P, T], U8, name="x_byte_table", align_bytes=64)
         d_word_table = keep.tile([P, G], U32, name="d_word_table", align_bytes=64)
         x_word_table = keep.tile([P, T], U32, name="x_word_table", align_bytes=64)
-        k1_list = load_list("k1_list", k1)
-        nc.sync.dma_start(
-            d_byte_table[:].bitcast(I32), d_scales[0].bitcast(I32).unsqueeze(1).to_broadcast([16, 8, G // 4])
-        )
         offs_list = load_list("offs_list", offs)
         nc.sync.dma_start(
             x_byte_table[:].bitcast(I32), x_scales[0].bitcast(I32).unsqueeze(1).to_broadcast([16, 8, T // 4])
+        )
+        k1_list = load_list("k1_list", k1)
+        nc.sync.dma_start(
+            d_byte_table[:].bitcast(I32), d_scales[0].bitcast(I32).unsqueeze(1).to_broadcast([16, 8, G // 4])
         )
         nc.sync.dma_start(x_word_table[:].bitcast(I32), x_words[0].rearrange("p n t -> p (n t)").bitcast(I32))
         load_w1(0)
@@ -122,13 +122,13 @@ def tile_picked_twpqcxbelg_none_p_kernel(
             nc.vector.memset(placed[:].bitcast(I32), 0)
             dealt = keep.tile([P, H + S], U8, name=name + "_dealt", align_bytes=64)
             d_dealt = keep.tile([P, H], U32, name=name + "_d_dealt", align_bytes=64)
-            nc.vector.tensor_copy(picked[:, 0:H], d_byte_table[:].indirect(d_list[:]))
             nc.vector.tensor_copy(picked[:, H : H + S], x_byte_table[:].indirect(x_list[:]))
+            nc.vector.tensor_copy(picked[:, 0:H], d_byte_table[:].indirect(d_list[:]))
+            nc.vector.tensor_copy(dealt[:, H : H + S].bitcast(I32), picked[:, H : H + S].bitcast(I32))
             nc.vector.tensor_copy(
                 dealt[:, 0:H].rearrange("p (t c i) -> p c t i", t=PACK, i=16),
                 picked[:, 0:H].rearrange("p (c i t) -> p c t i", t=PACK, i=16),
             )
-            nc.vector.tensor_copy(dealt[:, H : H + S].bitcast(I32), picked[:, H : H + S].bitcast(I32))
             for r in range(4):
                 queue.dma_start(placed[r:P:32, :].bitcast(I32), dealt[8 * r : P : 32, :].bitcast(I32))
             nc.vector.tensor_copy(x_picked[:], x_word_table[:].indirect(x_list[:]))
@@ -155,7 +155,7 @@ def tile_picked_twpqcxbelg_none_p_kernel(
         a_d_picked = reuse.tile([P, H], U32, name="a_d_picked", align_bytes=64, offset=2048)
         a_banks = coded_product("a", k1_list, offs_list, a_picked, a_d_picked, a_x_picked, "first", nc.scalar)
 
-        sg = []
+        sg, gained = [], []
         for t in range(PACK):
             a_rows = reuse.tile([P, S], F32, name="a_rows%d" % t, offset=12288 + 4 * S * t)
             nc.scalar.activation(a_rows[:], a_banks[t][:], ACT.Copy, scale=0.0625)
@@ -166,6 +166,11 @@ def tile_picked_twpqcxbelg_none_p_kernel(
                     bias=bias_a[:, t : t + 1], scale=sl_rows[:, t : t + 1],
                 )
             sg.append(gate)
+            gained_gate = keep.tile([P, HALF], F32, name="gained%d" % t)
+            nc.gpsimd.tensor_scalar(
+                gained_gate[:], gate[:, half_cols(1)], gn_rows[:, t : t + 1], 0.0, ALU.mult, ALU.add
+            )
+            gained.append(gained_gate)
 
         b_d_picked = reuse.tile([P, H], U32, name="b_d_picked", align_bytes=64, offset=256)
         b_picked = reuse.tile([P, H + S], U8, name="b_picked", align_bytes=64, offset=2304)
@@ -177,17 +182,21 @@ def tile_picked_twpqcxbelg_none_p_kernel(
         w_codes = keep.tile([P, N], U32, name="w_codes", align_bytes=64)
         w_bytes = keep.tile([P, N], U8, name="w_bytes", align_bytes=64)
         nc.vector.quantize_mx(out=w_codes[:].bitcast(FP8X4), scales=w_bytes[:], in_=w_grouped[:])
-        for t in range(PACK - 1):
+        for t in range(PACK):
             nc.vector.tensor_scalar(b_rows[t][:], b_banks[t][:], 0.0625, None, ALU.mult)
-        nc.scalar.activation(b_rows[PACK - 1][:], b_banks[PACK - 1][:], ACT.Copy, scale=0.0625)
 
-        first_term = reuse.tile([P, PACK, S], F32, name="first_term", offset=3328)
+        first_term = [
+            reuse.tile([P, PACK, HALF], F32, name="first_term0", offset=3328),
+            keep.tile([P, PACK, HALF], F32, name="first_term1"),
+        ]
         for t in range(PACK):
             nc.vector.scalar_tensor_tensor(
-                first_term[:, t, :], b_banks[t][:], gain[:, t : t + 1], sg[t][:], ALU.mult, ALU.mult
+                first_term[0][:, t, :], b_banks[t][:, half_cols(0)], gain[:, t : t + 1], sg[t][:, half_cols(0)],
+                ALU.mult, ALU.mult,
             )
+            nc.gpsimd.tensor_tensor(first_term[1][:, t, :], gained[t][:], b_rows[t][:, half_cols(1)], ALU.mult)
 
-        h_banks = [psum.tile([P, S], F32, name="h_sums%d" % t, tag="second%d" % t) for t in range(PACK)]
+        h_banks = []
         for half in HALVES:
             cols = half_cols(half)
             second_term = keep.tile(
@@ -205,7 +214,7 @@ def tile_picked_twpqcxbelg_none_p_kernel(
             z_grouped = keep.tile([P, HALF * PACK], BF16, name="z_grouped%d" % half, tag="stage%d" % (half + 1), align_bytes=64)
             nc.vector.tensor_tensor(
                 z_grouped[:].rearrange("p (c i t) -> p c t i", t=PACK, i=4),
-                first_term[:, :, cols].rearrange("p t (c i) -> p c t i", i=4),
+                first_term[half][:].rearrange("p t (c i) -> p c t i", i=4),
                 second_term[:].rearrange("p t (c i) -> p c t i", i=4),
                 ALU.add,
             )
@@ -214,8 +223,10 @@ def tile_picked_twpqcxbelg_none_p_kernel(
             nc.vector.quantize_mx(out=z_codes[:].bitcast(FP8X4), scales=z_bytes[:], in_=z_grouped[:])
             for t in range(PACK):
                 rows = slice(t * P, (t + 1) * P)
+                bank = psum.tile([P, HALF], F32, name="h_sums%d_%d" % (half, t), tag=("second%d", "first%d")[half] % t)
+                h_banks.append(bank)
                 nc.tensor.matmul_mx(
-                    out=h_banks[t][:, cols],
+                    out=bank[:],
                     lhsT=w_codes[:, rows].bitcast(FP8X4), lhsT_scale=w_bytes[:, rows],
                     rhs=z_codes[:].bitcast(FP8X4), rhs_scale=z_bytes[:],
                     start=True, stop=True,
@@ -223,9 +234,15 @@ def tile_picked_twpqcxbelg_none_p_kernel(
 
         h_rows, exp_bias = [], []
         for t in range(PACK):
-            rows = keep.tile([P, S], F32, name="h_rows%d" % t)
-            top = keep.tile([P, 1], F32, name="top%d" % t)
-            nc.vector.tensor_scalar(rows[:], h_banks[t][:], 1.0, None, ALU.mult, ALU.max, accum_out=top[:])
+            rows = keep.tile([P, S], F32, name="h_rows%d" % t, tag="h_rows%d" % t)
+            top = keep.tile([P, 1], F32, name="top%d" % t, tag="h_rows%d" % (t + 1))
+            half_top = keep.tile([P, 1], F32, name="half_top%d" % t)
+            nc.vector.tensor_scalar(
+                rows[:, half_cols(0)], h_banks[t][:], 1.0, None, ALU.mult, ALU.max, accum_out=half_top[:]
+            )
+            nc.vector.tensor_scalar(
+                rows[:, half_cols(1)], h_banks[PACK + t][:], 1.0, half_top[:], ALU.mult, ALU.max, accum_out=top[:]
+            )
             bias = keep.tile([P, 1], F32, name="exp_bias%d" % t)
             nc.vector.tensor_tensor(bias[:], top[:], minus_tau[:, t : t + 1], ALU.mult)
             h_rows.append(rows)

@@ -157,14 +157,13 @@ def tile_picked_twpqcxbelg_none_p_kernel(
 
         sg, gained = [], []
         for t in range(PACK):
-            a_rows = reuse.tile([P, S], F32, name="a_rows%d" % t, offset=12288 + 4 * S * t)
-            nc.scalar.activation(a_rows[:], a_banks[t][:], ACT.Copy, scale=0.0625)
+            a_rows = reuse.tile([P, 2 * S], F32, name="a_rows%d" % t, offset=12288 + 2048 + 8 * S * (t - 1))
+            nc.scalar.activation(a_rows[:, 0:S], a_banks[t][:], ACT.Copy, scale=0.0625)
             gate = keep.tile([P, S], F32, name="sg%d" % t, tag="sg%d" % t)
-            for half in HALVES:
-                nc.scalar.activation(
-                    gate[:, half_cols(half)], a_rows[:].indirect(half_list(n1_list, half)), ACT.Sigmoid,
-                    bias=bias_a[:, t : t + 1], scale=sl_rows[:, t : t + 1],
-                )
+            nc.scalar.activation(
+                gate[:], a_rows[:].indirect(n1_list[:]), ACT.Sigmoid,
+                bias=bias_a[:, t : t + 1], scale=sl_rows[:, t : t + 1],
+            )
             sg.append(gate)
             gained_gate = keep.tile([P, HALF], F32, name="gained%d" % t)
             nc.gpsimd.tensor_scalar(
@@ -234,7 +233,7 @@ def tile_picked_twpqcxbelg_none_p_kernel(
 
         h_rows, exp_bias = [], []
         for t in range(PACK):
-            rows = keep.tile([P, S], F32, name="h_rows%d" % t, tag="h_rows%d" % t)
+            rows = keep.tile([P, 2 * S], F32, name="h_rows%d" % t, tag="h_rows%d" % t)
             top = keep.tile([P, 1], F32, name="top%d" % t, tag="h_rows%d" % (t + 1))
             half_top = keep.tile([P, 1], F32, name="half_top%d" % t)
             nc.vector.tensor_scalar(
@@ -253,11 +252,10 @@ def tile_picked_twpqcxbelg_none_p_kernel(
             pair = []
             for which, place_list in enumerate((n3_list, n4_list)):
                 fetched = keep.tile([P, S], F32, name="ea%d_%d" % (which, t))
-                for half in HALVES:
-                    nc.scalar.activation(
-                        fetched[:, half_cols(half)], h_rows[t][:].indirect(half_list(place_list, half)), ACT.Exp,
-                        bias=exp_bias[t][:], scale=tau_rows[:, t : t + 1],
-                    )
+                nc.scalar.activation(
+                    fetched[:], h_rows[t][:].indirect(place_list[:]), ACT.Exp,
+                    bias=exp_bias[t][:], scale=tau_rows[:, t : t + 1],
+                )
                 pair.append(fetched)
             total = keep.tile([P, S], F32, name="total%d" % t)
             nc.vector.tensor_tensor(total[:], pair[0][:], pair[1][:], ALU.add)

from contextlib import ExitStack

import concourse.mybir as mybir

K, T, S, N, G, H = 512, 1024, 512, 512, 2048, 512
FLOPS = 2 * K * H * S * 2 + 2 * H * N * S

F32 = mybir.dt.float32
BF16 = mybir.dt.bfloat16
I32 = mybir.dt.int32
U32 = mybir.dt.uint32
U16 = mybir.dt.uint16
U8 = mybir.dt.uint8
FP8X4 = mybir.dt.float8_e4m3fn_x4
ALU = mybir.AluOpType
ACT = mybir.ActivationFunctionType

P = 128
PACK = 4
HALF = S // 2
LIST_COLS = S // 16
HALVES = (0, 1)


def tile_picked_twpqcxbelg_none_p_kernel(
    tc, x_words, x_scales, d_words, d_scales, sl, th, sl2, th2, gn, w1, tau,
    offs, k1, two, k2, n1, n2, n3, n4, out,
):
    nc = tc.nc
    with ExitStack() as ctx:
        lists = ctx.enter_context(tc.tile_pool(name="lists", bufs=1))
        keep = ctx.enter_context(tc.tile_pool(name="keep", bufs=1))
        reuse = ctx.enter_context(tc.tile_pool(name="reuse", bufs=1))
        psum = ctx.enter_context(tc.psum_pool(name="psum", bufs=1))

        def load_list(name, source):
            tile = lists.tile([P, LIST_COLS], U16, name=name)
            nc.sync.dma_start(tile[:], source)
            return tile

        w_raw = [
            reuse.tile([P, PACK, N // 2], F32, name="w_raw0", offset=12288),
            keep.tile([P, PACK, N // 2], F32, name="w_raw1"),
        ]

        def load_w1(half):
            columns = slice(half * N // 2, (half + 1) * N // 2)
            nc.sync.dma_start(w_raw[half][:], w1.rearrange("(p j) m -> p j m", j=PACK)[:, :, columns])

        def half_cols(half):
            return slice(half * HALF, (half + 1) * HALF)

        def half_list(tile, half):
            return tile[:, half * LIST_COLS // 2 : (half + 1) * LIST_COLS // 2]

        warm_in = keep.tile([P, 1], F32, name="warm_in")
        warm_out = keep.tile([P, 1], F32, name="warm_out")
        nc.vector.memset(warm_in[:], 0.0)
        nc.scalar.activation(warm_out[:], warm_in[:], ACT.Sigmoid)

        d_byte_table = keep.tile([P, G], U8, name="d_byte_table", align_bytes=64)
        x_byte_table = keep.tile([P, T], U8, name="x_byte_table", align_bytes=64)
        d_word_table = keep.tile([P, G], U32, name="d_word_table", align_bytes=64)
        x_word_table = keep.tile([P, T], U32, name="x_word_table", align_bytes=64)
        offs_list = load_list("offs_list", offs)
        nc.sync.dma_start(
            x_byte_table[:].bitcast(I32), x_scales[0].bitcast(I32).unsqueeze(1).to_broadcast([16, 8, T // 4])
        )
        k1_list = load_list("k1_list", k1)
        nc.sync.dma_start(
            d_byte_table[:].bitcast(I32), d_scales[0].bitcast(I32).unsqueeze(1).to_broadcast([16, 8, G // 4])
        )
        nc.sync.dma_start(x_word_table[:].bitcast(I32), x_words[0].rearrange("p n t -> p (n t)").bitcast(I32))
        load_w1(0)
        nc.sync.dma_start(d_word_table[:].bitcast(I32), d_words[0].rearrange("p n t -> p (n t)").bitcast(I32))
        k2_list = load_list("k2_list", k2)
        two_list = load_list("two_list", two)
        n1_list = load_list("n1_list", n1)
        n2_list = load_list("n2_list", n2)
        n3_list = load_list("n3_list", n3)
        n4_list = load_list("n4_list", n4)
        load_w1(1)
        w_grouped = keep.tile([P, N * PACK], BF16, name="w_grouped", align_bytes=64)

        def group_w1(copy, half):
            copy(
                w_grouped[:].rearrange("p (t h m j) -> p h m j t", t=PACK, h=2, j=PACK)[:, half],
                w_raw[half][:].rearrange("p j (m t) -> p m j t", t=PACK),
            )

        group_w1(nc.scalar.copy, 0)

        def load_rows(name, source):
            tile = keep.tile([P, PACK], F32, name=name)
            nc.gpsimd.dma_start(tile[:], source.rearrange("(p t) o -> p (t o)", t=PACK))
            return tile

        def times(name, tile, factor):
            result = keep.tile([P, PACK], F32, name=name)
            nc.gpsimd.tensor_scalar(result[:], tile[:], factor, 0.0, ALU.mult, ALU.add)
            return result

        def sigmoid_bias(name, slope, threshold):
            minus = times(name + "_minus", threshold, -1.0)
            result = keep.tile([P, PACK], F32, name=name)
            nc.gpsimd.tensor_tensor(result[:], slope[:], minus[:], ALU.mult)
            return result

        sl_rows = load_rows("sl_rows", sl)
        th_rows = load_rows("th_rows", th)
        bias_a = sigmoid_bias("bias_a", sl_rows, th_rows)
        sl2_rows = load_rows("sl2_rows", sl2)
        th2_rows = load_rows("th2_rows", th2)
        bias_b = sigmoid_bias("bias_b", sl2_rows, th2_rows)
        gn_rows = load_rows("gn_rows", gn)
        gain = times("gain", gn_rows, 0.0625)
        tau_rows = load_rows("tau_rows", tau)
        minus_tau = times("minus_tau", tau_rows, -1.0)

        def coded_product(name, d_list, x_list, picked, d_picked, x_picked, bank_tag, queue):
            placed = keep.tile([P, H + S], U8, name=name + "_placed", align_bytes=64)
            nc.vector.memset(placed[:].bitcast(I32), 0)
            dealt = keep.tile([P, H + S], U8, name=name + "_dealt", align_bytes=64)
            d_dealt = keep.tile([P, H], U32, name=name + "_d_dealt", align_bytes=64)
            nc.vector.tensor_copy(picked[:, H : H + S], x_byte_table[:].indirect(x_list[:]))
            nc.vector.tensor_copy(picked[:, 0:H], d_byte_table[:].indirect(d_list[:]))
            nc.vector.tensor_copy(dealt[:, H : H + S].bitcast(I32), picked[:, H : H + S].bitcast(I32))
            nc.vector.tensor_copy(
                dealt[:, 0:H].rearrange("p (t c i) -> p c t i", t=PACK, i=16),
                picked[:, 0:H].rearrange("p (c i t) -> p c t i", t=PACK, i=16),
            )
            for r in range(4):
                queue.dma_start(placed[r:P:32, :].bitcast(I32), dealt[8 * r : P : 32, :].bitcast(I32))
            nc.vector.tensor_copy(x_picked[:], x_word_table[:].indirect(x_list[:]))
            nc.vector.tensor_copy(d_picked[:], d_word_table[:].indirect(d_list[:]))
            nc.vector.tensor_copy(
                d_dealt[:].bitcast(I32).rearrange("p (t c i) -> p c t i", t=PACK, i=4),
                d_picked[:].bitcast(I32).rearrange("p (c i t) -> p c t i", t=PACK, i=4),
            )
            banks = []
            for t in range(PACK):
                bank = psum.tile([P, S], F32, name=name + "_sums%d" % t, tag=bank_tag + "%d" % t)
                cols = slice(t * P, (t + 1) * P)
                nc.tensor.matmul_mx(
                    out=bank[:],
                    lhsT=d_dealt[:, cols].bitcast(FP8X4), lhsT_scale=placed[:, cols],
                    rhs=x_picked[:].bitcast(FP8X4), rhs_scale=placed[:, H : H + S],
                    start=True, stop=True,
                )
                banks.append(bank)
            return banks

        a_picked = keep.tile([P, H + S], U8, name="a_picked", align_bytes=64)
        a_x_picked = keep.tile([P, S], U32, name="a_x_picked", align_bytes=64)
        a_d_picked = reuse.tile([P, H], U32, name="a_d_picked", align_bytes=64, offset=2048)
        a_banks = coded_product("a", k1_list, offs_list, a_picked, a_d_picked, a_x_picked, "first", nc.scalar)

        sg, gained = [], []
        for t in range(PACK):
            a_rows = reuse.tile([P, 2 * S], F32, name="a_rows%d" % t, offset=12288 + 2048 + 8 * S * (t - 1))
            nc.scalar.activation(a_rows[:, 0:S], a_banks[t][:], ACT.Copy, scale=0.0625)
            gate = keep.tile([P, S], F32, name="sg%d" % t, tag="sg%d" % t)
            nc.scalar.activation(
                gate[:], a_rows[:].indirect(n1_list[:]), ACT.Sigmoid,
                bias=bias_a[:, t : t + 1], scale=sl_rows[:, t : t + 1],
            )
            sg.append(gate)
            gained_gate = keep.tile([P, HALF], F32, name="gained%d" % t)
            nc.gpsimd.tensor_scalar(
                gained_gate[:], gate[:, half_cols(1)], gn_rows[:, t : t + 1], 0.0, ALU.mult, ALU.add
            )
            gained.append(gained_gate)

        b_d_picked = reuse.tile([P, H], U32, name="b_d_picked", align_bytes=64, offset=256)
        b_picked = reuse.tile([P, H + S], U8, name="b_picked", align_bytes=64, offset=2304)
        b_x_picked = reuse.tile([P, S], U32, name="b_x_picked", align_bytes=64, offset=3328)
        b_banks = coded_product("b", k2_list, two_list, b_picked, b_d_picked, b_x_picked, "second", nc.sync)

        b_rows = [keep.tile([P, S], F32, name="b_rows%d" % t) for t in range(PACK)]
        group_w1(nc.vector.tensor_copy, 1)
        w_codes = keep.tile([P, N], U32, name="w_codes", align_bytes=64)
        w_bytes = keep.tile([P, N], U8, name="w_bytes", align_bytes=64)
        nc.vector.quantize_mx(out=w_codes[:].bitcast(FP8X4), scales=w_bytes[:], in_=w_grouped[:])
        for t in range(PACK):
            nc.vector.tensor_scalar(b_rows[t][:], b_banks[t][:], 0.0625, None, ALU.mult)

        first_term = [
            reuse.tile([P, PACK, HALF], F32, name="first_term0", offset=3328),
            keep.tile([P, PACK, HALF], F32, name="first_term1"),
        ]
        for t in range(PACK):
            nc.vector.scalar_tensor_tensor(
                first_term[0][:, t, :], b_banks[t][:, half_cols(0)], gain[:, t : t + 1], sg[t][:, half_cols(0)],
                ALU.mult, ALU.mult,
            )
            nc.gpsimd.tensor_tensor(first_term[1][:, t, :], gained[t][:], b_rows[t][:, half_cols(1)], ALU.mult)

        h_banks = []
        for half in HALVES:
            cols = half_cols(half)
            second_term = keep.tile(
                [P, PACK, HALF], F32, name="second_term%d" % half, tag="stage%d" % half, align_bytes=64
            )
            for t in range(PACK):
                gate = keep.tile([P, HALF], F32, name="sg2_%d_%d" % (half, t), tag=("sg2_%d", "sg%d")[half] % t)
                nc.scalar.activation(
                    gate[:], b_rows[t][:].indirect(half_list(n2_list, half)), ACT.Sigmoid,
                    bias=bias_b[:, t : t + 1], scale=sl2_rows[:, t : t + 1],
                )
                nc.vector.scalar_tensor_tensor(
                    second_term[:, t, :], a_banks[t][:, cols], gain[:, t : t + 1], gate[:], ALU.mult, ALU.mult
                )
            z_grouped = keep.tile([P, HALF * PACK], BF16, name="z_grouped%d" % half, tag="stage%d" % (half + 1), align_bytes=64)
            nc.vector.tensor_tensor(
                z_grouped[:].rearrange("p (c i t) -> p c t i", t=PACK, i=4),
                first_term[half][:].rearrange("p t (c i) -> p c t i", i=4),
                second_term[:].rearrange("p t (c i) -> p c t i", i=4),
                ALU.add,
            )
            z_codes = keep.tile([P, HALF], U32, name="z_codes%d" % half, align_bytes=64)
            z_bytes = keep.tile([P, HALF], U8, name="z_bytes%d" % half, align_bytes=64)
            nc.vector.quantize_mx(out=z_codes[:].bitcast(FP8X4), scales=z_bytes[:], in_=z_grouped[:])
            for t in range(PACK):
                rows = slice(t * P, (t + 1) * P)
                bank = psum.tile([P, HALF], F32, name="h_sums%d_%d" % (half, t), tag=("second%d", "first%d")[half] % t)
                h_banks.append(bank)
                nc.tensor.matmul_mx(
                    out=bank[:],
                    lhsT=w_codes[:, rows].bitcast(FP8X4), lhsT_scale=w_bytes[:, rows],
                    rhs=z_codes[:].bitcast(FP8X4), rhs_scale=z_bytes[:],
                    start=True, stop=True,
                )

        h_rows, exp_bias = [], []
        for t in range(PACK):
            rows = keep.tile([P, 2 * S], F32, name="h_rows%d" % t, tag="h_rows%d" % t)
            top = keep.tile([P, 1], F32, name="top%d" % t, tag="h_rows%d" % (t + 1))
            half_top = keep.tile([P, 1], F32, name="half_top%d" % t)
            nc.vector.tensor_scalar(
                rows[:, half_cols(0)], h_banks[t][:], 1.0, None, ALU.mult, ALU.max, accum_out=half_top[:]
            )
            nc.vector.tensor_scalar(
                rows[:, half_cols(1)], h_banks[PACK + t][:], 1.0, half_top[:], ALU.mult, ALU.max, accum_out=top[:]
            )
            bias = keep.tile([P, 1], F32, name="exp_bias%d" % t)
            nc.vector.tensor_tensor(bias[:], top[:], minus_tau[:, t : t + 1], ALU.mult)
            h_rows.append(rows)
            exp_bias.append(bias)

        sums = []
        for t in range(PACK):
            pair = []
            for which, place_list in enumerate((n3_list, n4_list)):
                fetched = keep.tile([P, S], F32, name="ea%d_%d" % (which, t))
                nc.scalar.activation(
                    fetched[:], h_rows[t][:].indirect(place_list[:]), ACT.Exp,
                    bias=exp_bias[t][:], scale=tau_rows[:, t : t + 1],
                )
                pair.append(fetched)
            total = keep.tile([P, S], F32, name="total%d" % t)
            nc.vector.tensor_tensor(total[:], pair[0][:], pair[1][:], ALU.add)
            sums.append(total)

        out_rows = out.rearrange("(p t) j -> p t j", t=PACK)
        pieces = [(t, slice(0, S)) for t in range(PACK - 1)] + [(PACK - 1, half_cols(half)) for half in HALVES]
        for number, (t, cols) in enumerate(pieces):
            width = cols.stop - cols.start
            logs = keep.tile([P, width], F32, name="logs%d" % number)
            nc.scalar.activation(logs[:], sums[t][:, cols], ACT.Ln, bias=0.25)
            result = keep.tile([P, width], F32, name="result%d" % number)
            nc.vector.tensor_tensor(result[:], logs[:], h_rows[t][:, cols], ALU.add)
            nc.sync.dma_start(out_rows[:, t, cols], result[:])
